import numpy as np, ml_dtypes
CORES = [32,160,288,416,80,208,336,464]
N = 8
S, B = 3, 64
def setup_inputs(rng):
    return {"x": rng.standard_normal((N, 128, S * B), dtype=np.float32).astype(ml_dtypes.bfloat16), "gate": (0.9375 + 0.03125 * rng.standard_normal((N, 128, S * B), dtype=np.float32)).astype(ml_dtypes.bfloat16)}
def setup_inputs_big(rng):
    d = setup_inputs(rng)
    for k in ("x",): d[k] = (d[k].astype(np.float32) * 1048576.0).astype(d[k].dtype)
    return d
def setup_inputs_small(rng):
    d = setup_inputs(rng)
    for k in ("x",): d[k] = (d[k].astype(np.float32) * (1 / 1048576.0)).astype(d[k].dtype)
    return d
def setup_inputs_apart(rng):
    d = setup_inputs(rng)
    f = (10.0 ** rng.permutation(np.linspace(-1.5, 1.5, N))).astype(np.float32).reshape(N, 1, 1)
    for k in ("x",): d[k] = (d[k].astype(np.float32) * f).astype(d[k].dtype)
    return d
def reference(x, gate):
    X, GATE = x.astype(np.float64), gate.astype(np.float64)
    y = np.zeros((N, 128, S * B)); h = np.zeros((128, B))
    for r in range(N):
        for s in range(S):
            h = GATE[r][:, B * s:B * s + B] * h + X[r][:, B * s:B * s + B]
            y[r][:, B * s:B * s + B] = h
    return {"y": y.astype(ml_dtypes.bfloat16)}

@@ -1,0 +1,206 @@
+from concourse.bass import DstId, RemoteDMATransfer
+from concourse.mybir import AluOpType
+
+B = 64
+
+SCRATCH = {
+    "W": ("sbuf", [128, 4 * B], "bfloat16"),
+    "G": ("sbuf", [128, 3 * B], "bfloat16"),
+    "land": ("sbuf", [128, 7 * B], "bfloat16"),
+    "snd": ("sbuf", [128, 2 * B], "bfloat16"),
+    "LF": ("sbuf", [128, 3 * B], "bfloat16"),
+    "hs": ("sbuf", [128, B], "float32"),
+    "Y": ("sbuf", [128, 3 * B], "bfloat16"),
+    "pa": ("psum", [128, 8 * B], "float32"),
+    "pb": ("psum", [128, 8 * B], "float32"),
+}
+SLOT = {"C1": (0, 2 * B), "C3": (0, 2 * B), "C4": (0, 2 * B), "C5": (0, 2 * B), "C2": (2 * B, 2 * B), "C6": (2 * B, 2 * B),
+        "K234": (4 * B, 2 * B), "K34": (4 * B, 2 * B), "b0": (6 * B, B), "H1": (6 * B, B), "H2": (6 * B, B)}
+SEMAPHORES = ["ld", "v", "st", "ls"] + ["s_" + m for m in sorted(SLOT)]
+ROUND1 = {0: ("b0", (1, 5)), 1: ("C1", (0, 5)), 2: ("C2", (3, 5)), 3: ("C3", (4,)), 4: ("C4", (3,)), 5: ("C5", (6,)),
+          6: ("C6", (7,))}
+
+
+def rank_program(g, core, T, topo):
+    r = T.rank_of(core)
+    if r is None:
+        return
+    v, sem = g.vector, T.sem
+    MUL, ADD = AluOpType.mult, AluOpType.add
+    W, G, pa, pb = T.W, T.G, T.pa, T.pb
+    x0, x1, x2 = (W[:, s * B:(s + 1) * B] for s in range(3))
+    g0, g1, g2 = (G[:, s * B:(s + 1) * B] for s in range(3))
+    Wb, WA, L = W[:, 2 * B:3 * B], W[:, 3 * B:4 * B], W[:, 0:3 * B]
+    PT = [pb[:, s * B:(s + 1) * B] for s in range(3)]
+    M = [pa[:, s * B:(s + 1) * B] for s in range(3)]
+    t0, t1, t2, t3, t4 = (pa[:, k * B:(k + 1) * B] for k in range(3, 8))
+    u0, u1, u2 = (pb[:, k * B:(k + 1) * B] for k in range(3, 6))
+    nv, nls = [0], [0]
+
+    def _done(ins):
+        ins.then_inc(sem.v, 1)
+        nv[0] += 1
+        return nv[0]
+
+    def tt(out, a, b, op):
+        if nv[0]:
+            v.wait_ge(sem.v, nv[0])
+        return _done(v.tensor_tensor(out, a, b, op))
+
+    def cp(out, a):
+        if nv[0]:
+            v.wait_ge(sem.v, nv[0])
+        return _done(v.tensor_copy(out, a))
+
+    def landed(m):
+        c, w = SLOT[m]
+        if w == B:
+            return T.land[:, c:c + B]
+        return T.land[:, c:c + B], T.land[:, c + B:c + 2 * B]
+
+    def arrived(q, m):
+        q.wait_ge(sem["s_" + m], nbits(usable))
+
+    def nbits(m):
+        return bin(m).count("1")
+
+    usable = 0
+    for d in T.cores:
+        if d != core and topo.may_write(core, d):
+            usable = topo.mask(core, d) if not usable else usable & topo.mask(core, d)
+
+    def send(src, m, ranks):
+        c, w = SLOT[m]
+        dsts = [T.cores[k] for k in ranks]
+        for d in dsts:
+            if not topo.may_write(core, d):
+                raise ValueError("the plan asks for a write that the machine refuses")
+        ad = [topo.addr(d, core) for d in dsts]
+        if len(dsts) == 1:
+            g.remote_dma(T.land[:, c:c + w], src, sem["s_" + m], sem.ls, ad[0][1], ad[0][0], usable)
+        else:
+            g.remote_dma_fused([RemoteDMATransfer(dst_ids=[DstId(rid=a[0], pnc=a[1]) for a in ad], dma_engine_mask=usable,
+                                                  remote_sem=sem["s_" + m], srcs=[src],
+                                                  dsts=[T.land[:, c:c + w] for _ in ad], alu_op=0)], local_sem=sem.ls)
+        nls[0] += nbits(usable)
+
+    def fold(pair, Lsrc):
+        b, A = pair
+        for s in range(3):
+            tt(M[s], PT[s], b, MUL)
+        tt(T.LF[:, :], pa[:, 0:3 * B], Lsrc, ADD)
+        for s in range(3):
+            tt(PT[s], PT[s], A, MUL)
+
+    def final(h, Lsrc):
+        for s in range(3):
+            tt(M[s], PT[s], h, MUL)
+        store(T.Y[:, :], tt(T.Y[:, :], pa[:, 0:3 * B], Lsrc, ADD))
+
+    def store(src, after):
+        g.sync.wait_ge(sem.v, after)
+        g.sync.dma_start(T.y[:, :], src).then_inc(sem.st, 16)
+        g.sync.wait_ge(sem.st, 16)
+
+    g.sync.dma_start(L, T.x[:, :]).then_inc(sem.ld, 16)
+    g.scalar.dma_start(G[:, :], T.gate[:, :]).then_inc(sem.ld, 16)
+    v.wait_ge(sem.ld, 32)
+    tt(t0, g1, x0, MUL)
+    tt(t1, t0, x1, ADD)
+    tt(t2, t1, g2, MUL)
+    ready = tt(Wb, t2, x2, ADD)
+    if r > 0:
+        tt(PT[1], g0, g1, MUL)
+        ready = tt(WA, PT[1], g2, MUL)
+    if r in ROUND1:
+        m, ranks = ROUND1[r]
+        g.wait_ge(sem.v, ready)
+        send(Wb if r == 0 else W[:, 2 * B:4 * B], m, ranks)
+    lready = cp(x1, t1)
+    if r > 0:
+        cp(PT[0], g0)
+        tt(PT[2], PT[1], g2, MUL)
+
+    if r == 0:
+        store(L, lready)
+        cp(u1, Wb)
+        arrived(v, "C1")
+        b, A = landed("C1")
+        tt(t3, u1, A, MUL)
+        g.wait_ge(sem.v, tt(T.snd[:, 0:B], t3, b, ADD))
+        send(T.snd[:, 0:B], "H1", (3, 7))
+    elif r == 1:
+        arrived(v, "b0")
+        h = landed("b0")
+        tt(M[2], PT[2], h, MUL)
+        g.wait_ge(sem.v, tt(T.Y[:, 2 * B:3 * B], M[2], Wb, ADD))
+        send(T.Y[:, 2 * B:3 * B], "H1", (2, 6))
+        tt(M[0], PT[0], h, MUL)
+        tt(M[1], PT[1], h, MUL)
+        store(T.Y[:, :], tt(T.Y[:, 0:2 * B], pa[:, 0:2 * B], W[:, 0:2 * B], ADD))
+    elif r == 2:
+        arrived(v, "H1")
+        final(landed("H1"), L)
+    elif r == 3:
+        arrived(v, "C2")
+        b, A = landed("C2")
+        tt(t3, PT[2], b, MUL)
+        tt(t4, t3, Wb, ADD)
+        tt(u0, PT[2], A, MUL)
+        arrived(v, "C4")
+        b4, A4 = landed("C4")
+        tt(t3, t4, A4, MUL)
+        tt(T.snd[:, 0:B], t3, b4, ADD)
+        g.wait_ge(sem.v, tt(T.snd[:, B:2 * B], u0, A4, MUL))
+        send(T.snd[:, :], "K234", (6, 7))
+        fold((b, A), L)
+        arrived(v, "H1")
+        final(landed("H1"), T.LF[:, :])
+    elif r == 4:
+        arrived(v, "C3")
+        b, A = landed("C3")
+        tt(t3, PT[2], b, MUL)
+        tt(T.snd[:, 0:B], t3, Wb, ADD)
+        g.wait_ge(sem.v, tt(T.snd[:, B:2 * B], PT[2], A, MUL))
+        send(T.snd[:, :], "K34", (5,))
+        fold((b, A), L)
+        arrived(v, "H2")
+        final(landed("H2"), T.LF[:, :])
+    elif r == 5:
+        arrived(v, "b0")
+        arrived(v, "C1")
+        b, A = landed("C1")
+        tt(t3, A, landed("b0"), MUL)
+        tt(t4, t3, b, ADD)
+        arrived(v, "C2")
+        b, A = landed("C2")
+        tt(t3, t4, A, MUL)
+        g.wait_ge(sem.v, tt(T.snd[:, 0:B], t3, b, ADD))
+        send(T.snd[:, 0:B], "H2", (4,))
+        tt(u1, t3, b, ADD)
+        arrived(v, "K34")
+        b, A = landed("K34")
+        tt(t3, u1, A, MUL)
+        tt(T.hs[:, :], t3, b, ADD)
+        final(T.hs[:, :], L)
+    else:
+        if r == 6:
+            arrived(g, "C5")
+            c, w = SLOT["C5"]
+            send(T.land[:, c:c + w], "C5", (7,))
+            Lsrc = L
+        else:
+            arrived(v, "C6")
+            fold(landed("C6"), L)
+            Lsrc = T.LF[:, :]
+        arrived(v, "C5")
+        fold(landed("C5"), Lsrc)
+        arrived(v, "H1")
+        cp(u1, landed("H1"))
+        arrived(v, "K234")
+        b, A = landed("K234")
+        tt(t3, u1, A, MUL)
+        tt(T.hs[:, :], t3, b, ADD)
+        final(T.hs[:, :], T.LF[:, :])
+    if nls[0]:
+        g.wait_ge(sem.ls, nls[0])

@@ -6,19 +6,19 @@ B = 64
 SCRATCH = {
     "W": ("sbuf", [128, 4 * B], "bfloat16"),
     "G": ("sbuf", [128, 3 * B], "bfloat16"),
-    "land": ("sbuf", [128, 7 * B], "bfloat16"),
-    "snd": ("sbuf", [128, 2 * B], "bfloat16"),
+    "land": ("sbuf", [128, 13 * B], "bfloat16"),
+    "snd": ("sbuf", [128, B], "bfloat16"),
     "LF": ("sbuf", [128, 3 * B], "bfloat16"),
-    "hs": ("sbuf", [128, B], "float32"),
+    "hs": ("sbuf", [128, 2 * B], "float32"),
     "Y": ("sbuf", [128, 3 * B], "bfloat16"),
     "pa": ("psum", [128, 8 * B], "float32"),
     "pb": ("psum", [128, 8 * B], "float32"),
 }
-SLOT = {"C1": (0, 2 * B), "C3": (0, 2 * B), "C4": (0, 2 * B), "C5": (0, 2 * B), "C2": (2 * B, 2 * B), "C6": (2 * B, 2 * B),
-        "K234": (4 * B, 2 * B), "K34": (4 * B, 2 * B), "b0": (6 * B, B), "H1": (6 * B, B), "H2": (6 * B, B)}
+SLOT = {"C%d" % k: (2 * B * (k - 1), 2 * B) for k in range(1, 7)}
+SLOT.update({"b0": (12 * B, B), "H1": (12 * B, B), "H2": (12 * B, B)})
 SEMAPHORES = ["ld", "v", "st", "ls"] + ["s_" + m for m in sorted(SLOT)]
-ROUND1 = {0: ("b0", (1, 5)), 1: ("C1", (0, 5)), 2: ("C2", (3, 5)), 3: ("C3", (4,)), 4: ("C4", (3,)), 5: ("C5", (6,)),
-          6: ("C6", (7,))}
+ROUND1 = {0: ("b0", (1, 5)), 1: ("C1", (0, 5)), 2: ("C2", (5, 7, 6, 3)), 3: ("C3", (4, 7, 6)), 4: ("C4", (5, 7)),
+          5: ("C5", (6,)), 6: ("C6", (7,))}
 
 
 def rank_program(g, core, T, topo):
@@ -27,39 +27,55 @@ def rank_program(g, core, T, topo):
         return
     v, sem = g.vector, T.sem
     MUL, ADD = AluOpType.mult, AluOpType.add
-    W, G, pa, pb = T.W, T.G, T.pa, T.pb
-    x0, x1, x2 = (W[:, s * B:(s + 1) * B] for s in range(3))
-    g0, g1, g2 = (G[:, s * B:(s + 1) * B] for s in range(3))
-    Wb, WA, L = W[:, 2 * B:3 * B], W[:, 3 * B:4 * B], W[:, 0:3 * B]
-    PT = [pb[:, s * B:(s + 1) * B] for s in range(3)]
-    M = [pa[:, s * B:(s + 1) * B] for s in range(3)]
-    t0, t1, t2, t3, t4 = (pa[:, k * B:(k + 1) * B] for k in range(3, 8))
-    u0, u1, u2 = (pb[:, k * B:(k + 1) * B] for k in range(3, 6))
-    nv, nls = [0], [0]
 
-    def _done(ins):
-        ins.then_inc(sem.v, 1)
+    def blk(name, k, n=1):
+        return (name, k * B, (k + n) * B)
+
+    def ap(o):
+        return T[o[0]][:, o[1]:o[2]]
+
+    x0, x1, x2, WA = (blk("W", k) for k in range(4))
+    Wb, L, LF, Y = x2, blk("W", 0, 3), blk("LF", 0, 3), blk("Y", 0, 3)
+    g0, g1, g2 = (blk("G", k) for k in range(3))
+    PT = [blk("pb", s) for s in range(3)]
+    M = [blk("pa", s) for s in range(3)]
+    t0, t1, t2, t3, t4 = (blk("pa", k) for k in range(3, 8))
+    u0, u1, u2, u3, u4 = (blk("pb", k) for k in range(3, 8))
+    hs, kb = blk("hs", 0), blk("hs", 1)
+    snd = blk("snd", 0)
+    nv, nls, pend, force = [0], [0], [], [False]
+
+    def _ov(a, b):
+        return a[0] == b[0] and a[1] < b[2] and b[1] < a[2]
+
+    def _vec(out, ins, emit):
+        clash = force[0]
+        for w, rs in pend:
+            clash = clash or _ov(out, w) or any(_ov(out, q) for q in rs) or any(_ov(i, w) for i in ins)
+        if clash:
+            v.wait_ge(sem.v, nv[0])
+            del pend[:]
+            force[0] = False
+        emit().then_inc(sem.v, 1)
+        pend.append((out, ins))
         nv[0] += 1
         return nv[0]
 
     def tt(out, a, b, op):
-        if nv[0]:
-            v.wait_ge(sem.v, nv[0])
-        return _done(v.tensor_tensor(out, a, b, op))
+        return _vec(out, (a, b), lambda: v.tensor_tensor(ap(out), ap(a), ap(b), op))
 
     def cp(out, a):
-        if nv[0]:
-            v.wait_ge(sem.v, nv[0])
-        return _done(v.tensor_copy(out, a))
+        return _vec(out, (a,), lambda: v.tensor_copy(ap(out), ap(a)))
+
+    def told(q, n):
+        force[0] = True
+        q.wait_ge(sem.v, n)
 
     def landed(m):
         c, w = SLOT[m]
         if w == B:
-            return T.land[:, c:c + B]
-        return T.land[:, c:c + B], T.land[:, c + B:c + 2 * B]
-
-    def arrived(q, m):
-        q.wait_ge(sem["s_" + m], nbits(usable))
+            return ("land", c, c + B)
+        return ("land", c, c + B), ("land", c + B, c + 2 * B)
 
     def nbits(m):
         return bin(m).count("1")
@@ -69,6 +85,9 @@ def rank_program(g, core, T, topo):
         if d != core and topo.may_write(core, d):
             usable = topo.mask(core, d) if not usable else usable & topo.mask(core, d)
 
+    def arrived(q, m):
+        q.wait_ge(sem["s_" + m], nbits(usable))
+
     def send(src, m, ranks):
         c, w = SLOT[m]
         dsts = [T.cores[k] for k in ranks]
@@ -77,45 +96,59 @@ def rank_program(g, core, T, topo):
                 raise ValueError("the plan asks for a write that the machine refuses")
         ad = [topo.addr(d, core) for d in dsts]
         if len(dsts) == 1:
-            g.remote_dma(T.land[:, c:c + w], src, sem["s_" + m], sem.ls, ad[0][1], ad[0][0], usable)
+            g.remote_dma(T.land[:, c:c + w], ap(src), sem["s_" + m], sem.ls, ad[0][1], ad[0][0], usable)
         else:
             g.remote_dma_fused([RemoteDMATransfer(dst_ids=[DstId(rid=a[0], pnc=a[1]) for a in ad], dma_engine_mask=usable,
-                                                  remote_sem=sem["s_" + m], srcs=[src],
+                                                  remote_sem=sem["s_" + m], srcs=[ap(src)],
                                                   dsts=[T.land[:, c:c + w] for _ in ad], alu_op=0)], local_sem=sem.ls)
         nls[0] += nbits(usable)
 
-    def fold(pair, Lsrc):
-        b, A = pair
+    def pass_on(m, ranks):
+        arrived(g, m)
+        c, w = SLOT[m]
+        send(("land", c, c + w), m, ranks)
+
+    def fold(m, Lsrc):
+        arrived(v, m)
+        b, A = landed(m)
         for s in range(3):
             tt(M[s], PT[s], b, MUL)
-        tt(T.LF[:, :], pa[:, 0:3 * B], Lsrc, ADD)
+        tt(LF, blk("pa", 0, 3), Lsrc, ADD)
         for s in range(3):
             tt(PT[s], PT[s], A, MUL)
+
+    def onto(m, lo_b, lo_A, out_b, out_A, tmp):
+        arrived(v, m)
+        b, A = landed(m)
+        tt(tmp, lo_b, A, MUL)
+        tt(out_A, lo_A, A, MUL)
+        tt(out_b, tmp, b, ADD)
+
+    def store(src, after):
+        told(g.sync, after)
+        g.sync.dma_start(T.y[:, :], ap(src)).then_inc(sem.st, 16)
+        g.sync.wait_ge(sem.st, 16)
 
     def final(h, Lsrc):
         for s in range(3):
             tt(M[s], PT[s], h, MUL)
-        store(T.Y[:, :], tt(T.Y[:, :], pa[:, 0:3 * B], Lsrc, ADD))
+        store(Y, tt(Y, blk("pa", 0, 3), Lsrc, ADD))
 
-    def store(src, after):
-        g.sync.wait_ge(sem.v, after)
-        g.sync.dma_start(T.y[:, :], src).then_inc(sem.st, 16)
-        g.sync.wait_ge(sem.st, 16)
-
-    g.sync.dma_start(L, T.x[:, :]).then_inc(sem.ld, 16)
-    g.scalar.dma_start(G[:, :], T.gate[:, :]).then_inc(sem.ld, 16)
+    g.sync.dma_start(ap(L), T.x[:, :]).then_inc(sem.ld, 16)
+    g.scalar.dma_start(T.G[:, :], T.gate[:, :]).then_inc(sem.ld, 16)
     v.wait_ge(sem.ld, 32)
     tt(t0, g1, x0, MUL)
-    tt(t1, t0, x1, ADD)
-    tt(t2, t1, g2, MUL)
-    ready = tt(Wb, t2, x2, ADD)
     if r > 0:
         tt(PT[1], g0, g1, MUL)
-        ready = tt(WA, PT[1], g2, MUL)
+    tt(t1, t0, x1, ADD)
+    if r > 0:
+        tt(WA, PT[1], g2, MUL)
+    tt(t2, t1, g2, MUL)
+    ready = tt(Wb, t2, x2, ADD)
     if r in ROUND1:
         m, ranks = ROUND1[r]
-        g.wait_ge(sem.v, ready)
-        send(Wb if r == 0 else W[:, 2 * B:4 * B], m, ranks)
+        told(g, ready)
+        send(Wb if r == 0 else blk("W", 2, 2), m, ranks)
     lready = cp(x1, t1)
     if r > 0:
         cp(PT[0], g0)
@@ -127,46 +160,31 @@ def rank_program(g, core, T, topo):
         arrived(v, "C1")
         b, A = landed("C1")
         tt(t3, u1, A, MUL)
-        g.wait_ge(sem.v, tt(T.snd[:, 0:B], t3, b, ADD))
-        send(T.snd[:, 0:B], "H1", (3, 7))
+        told(g, tt(snd, t3, b, ADD))
+        send(snd, "H1", (7, 3))
     elif r == 1:
         arrived(v, "b0")
         h = landed("b0")
         tt(M[2], PT[2], h, MUL)
-        g.wait_ge(sem.v, tt(T.Y[:, 2 * B:3 * B], M[2], Wb, ADD))
-        send(T.Y[:, 2 * B:3 * B], "H1", (2, 6))
+        told(g, tt(blk("Y", 2), M[2], Wb, ADD))
+        send(blk("Y", 2), "H1", (6, 2))
         tt(M[0], PT[0], h, MUL)
         tt(M[1], PT[1], h, MUL)
-        store(T.Y[:, :], tt(T.Y[:, 0:2 * B], pa[:, 0:2 * B], W[:, 0:2 * B], ADD))
+        store(Y, tt(blk("Y", 0, 2), blk("pa", 0, 2), blk("W", 0, 2), ADD))
     elif r == 2:
         arrived(v, "H1")
         final(landed("H1"), L)
     elif r == 3:
-        arrived(v, "C2")
-        b, A = landed("C2")
-        tt(t3, PT[2], b, MUL)
-        tt(t4, t3, Wb, ADD)
-        tt(u0, PT[2], A, MUL)
-        arrived(v, "C4")
-        b4, A4 = landed("C4")
-        tt(t3, t4, A4, MUL)
-        tt(T.snd[:, 0:B], t3, b4, ADD)
-        g.wait_ge(sem.v, tt(T.snd[:, B:2 * B], u0, A4, MUL))
-        send(T.snd[:, :], "K234", (6, 7))
-        fold((b, A), L)
+        fold("C2", L)
         arrived(v, "H1")
-        final(landed("H1"), T.LF[:, :])
+        final(landed("H1"), LF)
     elif r == 4:
-        arrived(v, "C3")
-        b, A = landed("C3")
-        tt(t3, PT[2], b, MUL)
-        tt(T.snd[:, 0:B], t3, Wb, ADD)
-        g.wait_ge(sem.v, tt(T.snd[:, B:2 * B], PT[2], A, MUL))
-        send(T.snd[:, :], "K34", (5,))
-        fold((b, A), L)
+        pass_on("C3", (5,))
+        fold("C3", L)
         arrived(v, "H2")
-        final(landed("H2"), T.LF[:, :])
+        final(landed("H2"), LF)
     elif r == 5:
+        pass_on("C4", (6,))
         arrived(v, "b0")
         arrived(v, "C1")
         b, A = landed("C1")
@@ -175,32 +193,33 @@ def rank_program(g, core, T, topo):
         arrived(v, "C2")
         b, A = landed("C2")
         tt(t3, t4, A, MUL)
-        g.wait_ge(sem.v, tt(T.snd[:, 0:B], t3, b, ADD))
-        send(T.snd[:, 0:B], "H2", (4,))
         tt(u1, t3, b, ADD)
-        arrived(v, "K34")
-        b, A = landed("K34")
+        told(g, tt(snd, t3, b, ADD))
+        send(snd, "H2", (4,))
+        fold("C4", L)
+        arrived(v, "C3")
+        b, A = landed("C3")
         tt(t3, u1, A, MUL)
-        tt(T.hs[:, :], t3, b, ADD)
-        final(T.hs[:, :], L)
+        tt(hs, t3, b, ADD)
+        final(hs, LF)
     else:
         if r == 6:
-            arrived(g, "C5")
-            c, w = SLOT["C5"]
-            send(T.land[:, c:c + w], "C5", (7,))
-            Lsrc = L
+            pass_on("C5", (7,))
+            fold("C5", L)
         else:
-            arrived(v, "C6")
-            fold(landed("C6"), L)
-            Lsrc = T.LF[:, :]
-        arrived(v, "C5")
-        fold(landed("C5"), Lsrc)
+            fold("C6", L)
+        arrived(v, "C2")
+        b, A = landed("C2")
+        if r == 6:
+            onto("C3", b, A, u0, u1, t3)
+            onto("C4", u0, u1, kb, u3, t4)
+        else:
+            onto("C3", b, A, u0, u1, t3)
+            onto("C4", u0, u1, u2, u4, t4)
+            onto("C5", u2, u4, kb, u3, t3)
         arrived(v, "H1")
-        cp(u1, landed("H1"))
-        arrived(v, "K234")
-        b, A = landed("K234")
-        tt(t3, u1, A, MUL)
-        tt(T.hs[:, :], t3, b, ADD)
-        final(T.hs[:, :], T.LF[:, :])
+        tt(t2, u3, landed("H1"), MUL)
+        tt(hs, t2, kb, ADD)
+        final(hs, LF)
     if nls[0]:
         g.wait_ge(sem.ls, nls[0])

@@ -1,24 +1,32 @@
 from concourse.bass import DstId, RemoteDMATransfer
-from concourse.mybir import AluOpType
+from concourse.mybir import AluOpType, ActivationFunctionType
 
 B = 64
+SMAX = 9
 
 SCRATCH = {
-    "W": ("sbuf", [128, 4 * B], "bfloat16"),
+    "W": ("sbuf", [128, 3 * B], "bfloat16"),
     "G": ("sbuf", [128, 3 * B], "bfloat16"),
-    "land": ("sbuf", [128, 13 * B], "bfloat16"),
+    "PR": ("sbuf", [128, 2 * B], "bfloat16"),
+    "sw": ("sbuf", [128, B], "float32"),
     "snd": ("sbuf", [128, B], "bfloat16"),
-    "LF": ("sbuf", [128, 3 * B], "bfloat16"),
-    "hs": ("sbuf", [128, 2 * B], "float32"),
+    "land": ("sbuf", [128, 13 * B], "bfloat16"),
+    "D": ("sbuf", [128, 2 * B * SMAX], "bfloat16"),
+    "O": ("sbuf", [128, B * SMAX], "bfloat16"),
     "Y": ("sbuf", [128, 3 * B], "bfloat16"),
     "pa": ("psum", [128, 8 * B], "float32"),
-    "pb": ("psum", [128, 8 * B], "float32"),
 }
 SLOT = {"C%d" % k: (2 * B * (k - 1), 2 * B) for k in range(1, 7)}
-SLOT.update({"b0": (12 * B, B), "H1": (12 * B, B), "H2": (12 * B, B)})
-SEMAPHORES = ["ld", "v", "st", "ls"] + ["s_" + m for m in sorted(SLOT)]
-ROUND1 = {0: ("b0", (1, 5)), 1: ("C1", (0, 5)), 2: ("C2", (5, 7, 6, 3)), 3: ("C3", (4, 7, 6)), 4: ("C4", (5, 7)),
+SLOT.update({"b0": (12 * B, B), "H1": (12 * B, B)})
+SEMAPHORES = ["ldx", "ldg", "v", "a", "st", "ls"] + ["s_" + m for m in sorted(SLOT)]
+ROUND1 = {0: ("b0", (1, 5, 4)), 1: ("C1", (0, 5, 4)), 2: ("C2", (5, 7, 6, 3)), 3: ("C3", (4, 7, 6)), 4: ("C4", (5, 7)),
           5: ("C5", (6,)), 6: ("C6", (7,))}
+STATE = {0: (7, 3), 1: (6, 2)}
+PASS = {4: (("C3", (5,)),), 5: (("C4", (6,)), ("C2", (4,))), 6: (("C5", (7,)),)}
+SEQ = {1: ("b0",), 2: ("H1",), 3: ("H1", "C2"), 4: ("b0", "C1", "C2", "C3"), 5: ("b0", "C1", "C2", "C3", "C4"),
+       6: ("H1", "C2", "C3", "C4", "C5"), 7: ("H1", "C2", "C3", "C4", "C5", "C6")}
+DUE = {1: ("b0",), 2: ("H1",), 3: ("C2", "H1"), 4: ("C3", "b0", "C1", "C2"), 5: ("C4", "b0", "C1", "C2", "C3"),
+       6: ("C5", "C2", "C3", "C4", "H1"), 7: ("C6", "C4", "C2", "C3", "C5", "H1")}
 
 
 def rank_program(g, core, T, topo):
@@ -27,31 +35,31 @@ def rank_program(g, core, T, topo):
         return
     v, sem = g.vector, T.sem
     MUL, ADD = AluOpType.mult, AluOpType.add
+    S = len(SEQ[r]) + 3 if r else 0
 
-    def blk(name, k, n=1):
-        return (name, k * B, (k + n) * B)
+    def blk(nm, k, w=1):
+        return (nm, k * B, (k + w) * B, 1)
 
     def ap(o):
-        return T[o[0]][:, o[1]:o[2]]
+        if o[3] == 1:
+            return T[o[0]][:, o[1]:o[2]]
+        return T[o[0]][:, o[1]:o[2]:o[3]]
 
-    x0, x1, x2, WA = (blk("W", k) for k in range(4))
-    Wb, L, LF, Y = x2, blk("W", 0, 3), blk("LF", 0, 3), blk("Y", 0, 3)
+    x0, x1, x2 = (blk("W", k) for k in range(3))
     g0, g1, g2 = (blk("G", k) for k in range(3))
-    PT = [blk("pb", s) for s in range(3)]
-    M = [blk("pa", s) for s in range(3)]
-    t0, t1, t2, t3, t4 = (blk("pa", k) for k in range(3, 8))
-    u0, u1, u2, u3, u4 = (blk("pb", k) for k in range(3, 8))
-    hs, kb = blk("hs", 0), blk("hs", 1)
-    snd = blk("snd", 0)
+    p, q, u, t, a32 = (blk("pa", k) for k in range(5))
+    w_, snd = blk("sw", 0), blk("snd", 0)
     nv, nls, pend, force = [0], [0], [], [False]
 
     def _ov(a, b):
-        return a[0] == b[0] and a[1] < b[2] and b[1] < a[2]
+        if a[0] != b[0] or a[1] >= b[2] or b[1] >= a[2]:
+            return False
+        return not (a[3] == b[3] and a[3] > 1 and (a[1] - b[1]) % a[3])
 
     def _vec(out, ins, emit):
         clash = force[0]
-        for w, rs in pend:
-            clash = clash or _ov(out, w) or any(_ov(out, q) for q in rs) or any(_ov(i, w) for i in ins)
+        for wr, rs in pend:
+            clash = clash or _ov(out, wr) or any(_ov(out, k) for k in rs) or any(_ov(i, wr) for i in ins)
         if clash:
             v.wait_ge(sem.v, nv[0])
             del pend[:]
@@ -67,15 +75,9 @@ def rank_program(g, core, T, topo):
     def cp(out, a):
         return _vec(out, (a,), lambda: v.tensor_copy(ap(out), ap(a)))
 
-    def told(q, n):
+    def told(qu, k):
         force[0] = True
-        q.wait_ge(sem.v, n)
-
-    def landed(m):
-        c, w = SLOT[m]
-        if w == B:
-            return ("land", c, c + B)
-        return ("land", c, c + B), ("land", c + B, c + 2 * B)
+        qu.wait_ge(sem.v, k)
 
     def nbits(m):
         return bin(m).count("1")
@@ -85,8 +87,12 @@ def rank_program(g, core, T, topo):
         if d != core and topo.may_write(core, d):
             usable = topo.mask(core, d) if not usable else usable & topo.mask(core, d)
 
-    def arrived(q, m):
-        q.wait_ge(sem["s_" + m], nbits(usable))
+    def arrived(qu, m):
+        qu.wait_ge(sem["s_" + m], nbits(usable))
+
+    def landed(m):
+        c, w = SLOT[m]
+        return ("land", c, c + w, 1)
 
     def send(src, m, ranks):
         c, w = SLOT[m]
@@ -103,123 +109,66 @@ def rank_program(g, core, T, topo):
                                                   dsts=[T.land[:, c:c + w] for _ in ad], alu_op=0)], local_sem=sem.ls)
         nls[0] += nbits(usable)
 
-    def pass_on(m, ranks):
-        arrived(g, m)
-        c, w = SLOT[m]
-        send(("land", c, c + w), m, ranks)
-
-    def fold(m, Lsrc):
-        arrived(v, m)
-        b, A = landed(m)
-        for s in range(3):
-            tt(M[s], PT[s], b, MUL)
-        tt(LF, blk("pa", 0, 3), Lsrc, ADD)
-        for s in range(3):
-            tt(PT[s], PT[s], A, MUL)
-
-    def onto(m, lo_b, lo_A, out_b, out_A, tmp):
-        arrived(v, m)
-        b, A = landed(m)
-        tt(tmp, lo_b, A, MUL)
-        tt(out_A, lo_A, A, MUL)
-        tt(out_b, tmp, b, ADD)
-
     def store(src, after):
         told(g.sync, after)
         g.sync.dma_start(T.y[:, :], ap(src)).then_inc(sem.st, 16)
         g.sync.wait_ge(sem.st, 16)
 
-    def final(h, Lsrc):
-        for s in range(3):
-            tt(M[s], PT[s], h, MUL)
-        store(Y, tt(Y, blk("pa", 0, 3), Lsrc, ADD))
+    g.sync.dma_start(T.W[:, :], T.x[:, :]).then_inc(sem.ldx, 16)
+    c0 = 0 if r else B
+    g.scalar.dma_start(T.G[:, c0:], T.gate[:, c0:]).then_inc(sem.ldg, 16)
+    if r > 0:
+        z = ("D", B * S, 2 * B * S, S)
+        _vec(z, (), lambda: v.memset(ap(z), 0.0))
+    v.wait_ge(sem.ldg, 16)
 
-    g.sync.dma_start(ap(L), T.x[:, :]).then_inc(sem.ld, 16)
-    g.scalar.dma_start(T.G[:, :], T.gate[:, :]).then_inc(sem.ld, 16)
-    v.wait_ge(sem.ld, 32)
-    tt(t0, g1, x0, MUL)
-    if r > 0:
-        tt(PT[1], g0, g1, MUL)
-    tt(t1, t0, x1, ADD)
-    if r > 0:
-        tt(WA, PT[1], g2, MUL)
-    tt(t2, t1, g2, MUL)
-    ready = tt(Wb, t2, x2, ADD)
     if r in ROUND1:
-        m, ranks = ROUND1[r]
+        b_out = x2 if r == 0 else blk("PR", 0)
+        tt(p, g2, g1, MUL)
+        v.wait_ge(sem.ldx, 16)
+        tt(q, g2, x1, MUL)
+        tt(u, p, x0, MUL)
+        tt(w_, q, x2, ADD)
+        if r > 0:
+            tt(blk("PR", 1), p, g0, MUL)
+        ready = tt(b_out, u, w_, ADD)
         told(g, ready)
-        send(Wb if r == 0 else blk("W", 2, 2), m, ranks)
-    lready = cp(x1, t1)
-    if r > 0:
-        cp(PT[0], g0)
-        tt(PT[2], PT[1], g2, MUL)
+        send(b_out if r == 0 else blk("PR", 0, 2), ROUND1[r][0], ROUND1[r][1])
+    else:
+        v.wait_ge(sem.ldx, 16)
 
     if r == 0:
-        store(L, lready)
-        cp(u1, Wb)
+        tt(t, g1, x0, MUL)
+        store(blk("W", 0, 3), tt(x1, t, x1, ADD))
+        cp(q, x2)
         arrived(v, "C1")
-        b, A = landed("C1")
-        tt(t3, u1, A, MUL)
-        told(g, tt(snd, t3, b, ADD))
-        send(snd, "H1", (7, 3))
-    elif r == 1:
-        arrived(v, "b0")
-        h = landed("b0")
-        tt(M[2], PT[2], h, MUL)
-        told(g, tt(blk("Y", 2), M[2], Wb, ADD))
-        send(blk("Y", 2), "H1", (6, 2))
-        tt(M[0], PT[0], h, MUL)
-        tt(M[1], PT[1], h, MUL)
-        store(Y, tt(blk("Y", 0, 2), blk("pa", 0, 2), blk("W", 0, 2), ADD))
-    elif r == 2:
-        arrived(v, "H1")
-        final(landed("H1"), L)
-    elif r == 3:
-        fold("C2", L)
-        arrived(v, "H1")
-        final(landed("H1"), LF)
-    elif r == 4:
-        pass_on("C3", (5,))
-        fold("C3", L)
-        arrived(v, "H2")
-        final(landed("H2"), LF)
-    elif r == 5:
-        pass_on("C4", (6,))
-        arrived(v, "b0")
-        arrived(v, "C1")
-        b, A = landed("C1")
-        tt(t3, A, landed("b0"), MUL)
-        tt(t4, t3, b, ADD)
-        arrived(v, "C2")
-        b, A = landed("C2")
-        tt(t3, t4, A, MUL)
-        tt(u1, t3, b, ADD)
-        told(g, tt(snd, t3, b, ADD))
-        send(snd, "H2", (4,))
-        fold("C4", L)
-        arrived(v, "C3")
-        b, A = landed("C3")
-        tt(t3, u1, A, MUL)
-        tt(hs, t3, b, ADD)
-        final(hs, LF)
+        c = SLOT["C1"][0]
+        tt(u, q, ("land", c + B, c + 2 * B, 1), MUL)
+        told(g, tt(snd, u, ("land", c, c + B, 1), ADD))
+        send(snd, "H1", STATE[0])
     else:
-        if r == 6:
-            pass_on("C5", (7,))
-            fold("C5", L)
-        else:
-            fold("C6", L)
-        arrived(v, "C2")
-        b, A = landed("C2")
-        if r == 6:
-            onto("C3", b, A, u0, u1, t3)
-            onto("C4", u0, u1, kb, u3, t4)
-        else:
-            onto("C3", b, A, u0, u1, t3)
-            onto("C4", u0, u1, u2, u4, t4)
-            onto("C5", u2, u4, kb, u3, t3)
-        arrived(v, "H1")
-        tt(t2, u3, landed("H1"), MUL)
-        tt(hs, t2, kb, ADD)
-        final(hs, LF)
+        for m, ranks in PASS.get(r, ()):
+            arrived(g, m)
+            send(landed(m), m, ranks)
+        if r in STATE:
+            tt(a32, p, g0, MUL)
+        for s in range(3):
+            cp(("D", S - 3 + s, B * S, S), blk("W", s))
+            cp(("D", B * S + S - 3 + s, 2 * B * S, S), blk("G", s))
+        for m in DUE[r]:
+            arrived(v, m)
+            if r in STATE:
+                tt(t, a32, landed(m), MUL)
+                told(g, tt(snd, t, blk("PR", 0), ADD))
+                send(snd, "H1", STATE[r])
+            k = SEQ[r].index(m)
+            cp(("D", k, B * S if k == 0 else 2 * B * S, S), landed(m))
+        d1, d0, o = ("D", 0, B * S, 1), ("D", B * S, 2 * B * S, 1), ("O", 0, B * S, 1)
+        told(g.scalar, _vec(o, (d0, d1), lambda: v.tensor_tensor_scan(ap(o), ap(d0), ap(d1), 0.0, MUL, ADD)))
+        g.scalar.activation(ap(blk("Y", 2)), ap(("O", S - 1, B * S, S)), ActivationFunctionType.Copy).then_inc(sem.a, 1)
+        for s in range(2):
+            last = cp(blk("Y", s), ("O", S - 3 + s, B * S, S))
+        g.sync.wait_ge(sem.a, 1)
+        store(blk("Y", 0, 3), last)
     if nls[0]:
         g.wait_ge(sem.ls, nls[0])

from concourse.bass import DstId, RemoteDMATransfer
from concourse.mybir import AluOpType, ActivationFunctionType

B = 64
SMAX = 9

SCRATCH = {
    "W": ("sbuf", [128, 3 * B], "bfloat16"),
    "G": ("sbuf", [128, 3 * B], "bfloat16"),
    "PR": ("sbuf", [128, 2 * B], "bfloat16"),
    "sw": ("sbuf", [128, B], "float32"),
    "snd": ("sbuf", [128, B], "bfloat16"),
    "land": ("sbuf", [128, 13 * B], "bfloat16"),
    "D": ("sbuf", [128, 2 * B * SMAX], "bfloat16"),
    "O": ("sbuf", [128, B * SMAX], "bfloat16"),
    "Y": ("sbuf", [128, 3 * B], "bfloat16"),
    "pa": ("psum", [128, 8 * B], "float32"),
}
SLOT = {"C%d" % k: (2 * B * (k - 1), 2 * B) for k in range(1, 7)}
SLOT.update({"b0": (12 * B, B), "H1": (12 * B, B)})
SEMAPHORES = ["ldx", "ldg", "v", "a", "st", "ls"] + ["s_" + m for m in sorted(SLOT)]
ROUND1 = {0: ("b0", (1, 5, 4)), 1: ("C1", (0, 5, 4)), 2: ("C2", (5, 7, 6, 3)), 3: ("C3", (4, 7, 6)), 4: ("C4", (5, 7)),
          5: ("C5", (6,)), 6: ("C6", (7,))}
STATE = {0: (7, 3), 1: (6, 2)}
PASS = {4: (("C3", (5,)),), 5: (("C4", (6,)), ("C2", (4,))), 6: (("C5", (7,)),)}
SEQ = {1: ("b0",), 2: ("H1",), 3: ("H1", "C2"), 4: ("b0", "C1", "C2", "C3"), 5: ("b0", "C1", "C2", "C3", "C4"),
       6: ("H1", "C2", "C3", "C4", "C5"), 7: ("H1", "C2", "C3", "C4", "C5", "C6")}
DUE = {1: ("b0",), 2: ("H1",), 3: ("C2", "H1"), 4: ("C3", "b0", "C1", "C2"), 5: ("C4", "b0", "C1", "C2", "C3"),
       6: ("C5", "C2", "C3", "C4", "H1"), 7: ("C6", "C4", "C2", "C3", "C5", "H1")}


def rank_program(g, core, T, topo):
    r = T.rank_of(core)
    if r is None:
        return
    v, sem = g.vector, T.sem
    MUL, ADD = AluOpType.mult, AluOpType.add
    S = len(SEQ[r]) + 3 if r else 0

    def blk(nm, k, w=1):
        return (nm, k * B, (k + w) * B, 1)

    def ap(o):
        if o[3] == 1:
            return T[o[0]][:, o[1]:o[2]]
        return T[o[0]][:, o[1]:o[2]:o[3]]

    x0, x1, x2 = (blk("W", k) for k in range(3))
    g0, g1, g2 = (blk("G", k) for k in range(3))
    p, q, u, t, a32 = (blk("pa", k) for k in range(5))
    w_, snd = blk("sw", 0), blk("snd", 0)
    nv, nls, pend, force = [0], [0], [], [False]

    def _ov(a, b):
        if a[0] != b[0] or a[1] >= b[2] or b[1] >= a[2]:
            return False
        return not (a[3] == b[3] and a[3] > 1 and (a[1] - b[1]) % a[3])

    def _vec(out, ins, emit):
        clash = force[0]
        for wr, rs in pend:
            clash = clash or _ov(out, wr) or any(_ov(out, k) for k in rs) or any(_ov(i, wr) for i in ins)
        if clash:
            v.wait_ge(sem.v, nv[0])
            del pend[:]
            force[0] = False
        emit().then_inc(sem.v, 1)
        pend.append((out, ins))
        nv[0] += 1
        return nv[0]

    def tt(out, a, b, op):
        return _vec(out, (a, b), lambda: v.tensor_tensor(ap(out), ap(a), ap(b), op))

    def cp(out, a):
        return _vec(out, (a,), lambda: v.tensor_copy(ap(out), ap(a)))

    def told(qu, k):
        force[0] = True
        qu.wait_ge(sem.v, k)

    def nbits(m):
        return bin(m).count("1")

    usable = 0
    for d in T.cores:
        if d != core and topo.may_write(core, d):
            usable = topo.mask(core, d) if not usable else usable & topo.mask(core, d)

    def arrived(qu, m):
        qu.wait_ge(sem["s_" + m], nbits(usable))

    def landed(m):
        c, w = SLOT[m]
        return ("land", c, c + w, 1)

    def send(src, m, ranks):
        c, w = SLOT[m]
        dsts = [T.cores[k] for k in ranks]
        for d in dsts:
            if not topo.may_write(core, d):
                raise ValueError("the plan asks for a write that the machine refuses")
        ad = [topo.addr(d, core) for d in dsts]
        if len(dsts) == 1:
            g.remote_dma(T.land[:, c:c + w], ap(src), sem["s_" + m], sem.ls, ad[0][1], ad[0][0], usable)
        else:
            g.remote_dma_fused([RemoteDMATransfer(dst_ids=[DstId(rid=a[0], pnc=a[1]) for a in ad], dma_engine_mask=usable,
                                                  remote_sem=sem["s_" + m], srcs=[ap(src)],
                                                  dsts=[T.land[:, c:c + w] for _ in ad], alu_op=0)], local_sem=sem.ls)
        nls[0] += nbits(usable)

    def store(src, after):
        told(g.sync, after)
        g.sync.dma_start(T.y[:, :], ap(src)).then_inc(sem.st, 16)
        g.sync.wait_ge(sem.st, 16)

    g.sync.dma_start(T.W[:, :], T.x[:, :]).then_inc(sem.ldx, 16)
    c0 = 0 if r else B
    g.scalar.dma_start(T.G[:, c0:], T.gate[:, c0:]).then_inc(sem.ldg, 16)
    if r > 0:
        z = ("D", B * S, 2 * B * S, S)
        _vec(z, (), lambda: v.memset(ap(z), 0.0))
    v.wait_ge(sem.ldg, 16)

    if r in ROUND1:
        b_out = x2 if r == 0 else blk("PR", 0)
        tt(p, g2, g1, MUL)
        v.wait_ge(sem.ldx, 16)
        tt(q, g2, x1, MUL)
        tt(u, p, x0, MUL)
        tt(w_, q, x2, ADD)
        if r > 0:
            tt(blk("PR", 1), p, g0, MUL)
        ready = tt(b_out, u, w_, ADD)
        told(g, ready)
        send(b_out if r == 0 else blk("PR", 0, 2), ROUND1[r][0], ROUND1[r][1])
    else:
        v.wait_ge(sem.ldx, 16)

    if r == 0:
        tt(t, g1, x0, MUL)
        store(blk("W", 0, 3), tt(x1, t, x1, ADD))
        cp(q, x2)
        arrived(v, "C1")
        c = SLOT["C1"][0]
        tt(u, q, ("land", c + B, c + 2 * B, 1), MUL)
        told(g, tt(snd, u, ("land", c, c + B, 1), ADD))
        send(snd, "H1", STATE[0])
    else:
        for m, ranks in PASS.get(r, ()):
            arrived(g, m)
            send(landed(m), m, ranks)
        if r in STATE:
            tt(a32, p, g0, MUL)
        for s in range(3):
            cp(("D", S - 3 + s, B * S, S), blk("W", s))
            cp(("D", B * S + S - 3 + s, 2 * B * S, S), blk("G", s))
        for m in DUE[r]:
            arrived(v, m)
            if r in STATE:
                tt(t, a32, landed(m), MUL)
                told(g, tt(snd, t, blk("PR", 0), ADD))
                send(snd, "H1", STATE[r])
            k = SEQ[r].index(m)
            cp(("D", k, B * S if k == 0 else 2 * B * S, S), landed(m))
        d1, d0, o = ("D", 0, B * S, 1), ("D", B * S, 2 * B * S, 1), ("O", 0, B * S, 1)
        told(g.scalar, _vec(o, (d0, d1), lambda: v.tensor_tensor_scan(ap(o), ap(d0), ap(d1), 0.0, MUL, ADD)))
        g.scalar.activation(ap(blk("Y", 2)), ap(("O", S - 1, B * S, S)), ActivationFunctionType.Copy).then_inc(sem.a, 1)
        for s in range(2):
            last = cp(blk("Y", s), ("O", S - 3 + s, B * S, S))
        g.sync.wait_ge(sem.a, 1)
        store(blk("Y", 0, 3), last)
    if nls[0]:
        g.wait_ge(sem.ls, nls[0])
